import numpy as np
import ml_dtypes


def mxq(x, axis, fmt="e4m3"):
    dtype, down = {"e4m3": (ml_dtypes.float8_e4m3fn, 7), "e5m2": (ml_dtypes.float8_e5m2, 14)}[fmt]
    v = np.moveaxis(np.asarray(x, np.float32).astype(ml_dtypes.bfloat16).astype(np.float64), axis, -1)
    blocks = v.reshape(v.shape[:-1] + (-1, 32))
    amax = np.abs(blocks).max(-1, keepdims=True)
    byte = np.maximum(np.where(amax > 0, np.frexp(amax)[1] - 1 + 127, 0) - down, 1)
    scale = np.exp2(byte - 127.0)
    codes = (blocks / scale).astype(np.float32).astype(dtype).astype(np.float64)
    return np.moveaxis((codes * scale).reshape(v.shape), -1, axis)


WIDE = False


def mx_kscale(k):
    if not WIDE:
        return np.ones(k)
    levels = np.array([10, -10, 5, -5, 0])
    if k % 512:
        return np.exp2(np.random.permutation(np.resize(levels, k // 32))).repeat(32)
    a = np.empty((k // 512, 16))
    for p in range(k // 512):
        a[p, :8] = np.random.permutation(np.resize(levels, 8))
        for g in range(8):
            far = levels[np.abs(levels - a[p, g]) >= 10]
            a[p, g + 8] = far[np.random.randint(len(far))]
    return np.exp2(a.ravel()).repeat(32)


BF16 = ml_dtypes.bfloat16


def bf(x):
    return np.asarray(x, np.float32).astype(BF16)


def f64(x):
    return np.asarray(x).astype(np.float64)


T, D, F, R, E = 2048, 1024, 1024, 128, 8
ER = E * R


def draw0():
    u = mx_kscale(D)
    t = mx_kscale(ER)
    return {"x": bf(np.random.standard_normal((T, D)) * u),
            "w0": bf(np.random.standard_normal((D, F)) / np.sqrt(D) / u[:, None]),
            "wa": bf(np.random.standard_normal((D, R)) / np.sqrt(D) / u[:, None]),
            "c": bf(np.random.standard_normal((E, R))),
            "s": bf((1.0 + 0.1 * np.random.standard_normal(ER)) * t),
            "wb": bf(np.random.standard_normal((ER, F)) / np.sqrt(R) / t[:, None])}


def prototype_gate(a, c):
    diff = a[:, None, :] - c[None, :, :]
    logits = -np.sum(diff * diff, axis=-1) / 16.0
    e = np.exp(logits - logits.max(-1, keepdims=True))
    return e / e.sum(-1, keepdims=True)


def core(x, w0, wa, c, s, wb):
    xq = mxq(f64(x), 1, "e4m3")
    a = xq @ mxq(f64(wa), 0, "e4m3")
    g = prototype_gate(a, f64(c))
    z = (g[:, :, None] * a[:, None, :]).reshape(x.shape[0], wb.shape[0])
    zs = z * f64(s)[None, :]
    low = mxq(zs, 1, "e4m3") @ mxq(f64(wb), 0, "e4m3")
    return (xq @ mxq(f64(w0), 0, "e4m3")) + 1.5 * low


def e4m3fn_bytes(y):
    return np.clip(np.asarray(y, np.float64), -448.0, 448.0).astype(np.float32).astype(ml_dtypes.float8_e4m3fn).view(np.uint8)


def e4m3fn_values(b):
    return np.asarray(b, np.uint8).view(ml_dtypes.float8_e4m3fn).astype(np.float64)


def setup_inputs():
    d = draw0()
    x0 = np.asarray(d['x']).astype(np.float64)
    s = (np.max(np.abs(x0), axis=(0,), keepdims=True) / 448.0).astype(np.float32)
    out = {}
    for k, v in d.items():
        if k == 'x':
            out['x_bytes'] = e4m3fn_bytes(x0 / s.astype(np.float64))
            out['x_scale'] = s
        else:
            out[k] = v
    return out


def reference(x_bytes, x_scale, w0, wa, c, s, wb):
    return core(e4m3fn_values(x_bytes) * x_scale.astype(np.float64), w0, wa, c, s, wb)

@@ -1,0 +1,315 @@
+from contextlib import ExitStack
+
+import concourse.mybir as mybir
+from concourse.masks import make_identity
+
+T, D, F, R, E = 2048, 1024, 1024, 128, 8
+FLOPS = 2 * T * D * (F + R) + 2 * T * E * R * F
+
+F32 = mybir.dt.float32
+BF16 = mybir.dt.bfloat16
+U32 = mybir.dt.uint32
+U8 = mybir.dt.uint8
+FP8 = mybir.dt.float8_e4m3fn
+FP8X4 = mybir.dt.float8_e4m3fn_x4
+ALU = mybir.AluOpType
+ACT = mybir.ActivationFunctionType
+AX = mybir.AxisListType
+
+P = 128
+TILES = T // P
+X_GROUPS = [(0, 1), (1, 1), (2, 2), (4, 4), (8, 4), (12, 4)]
+BASE_LAG = 3
+LOW_LAG = 7
+W_PLAN = [("v", -2), ("s", -2), ("v", -1), ("s", -1), ("s", 0), ("s", 1), ("s", 2), ("s", 3)]
+
+
+def tile_hydraloraprototyperouted_kernel(tc, x_bytes, x_scale, w0, wa, c, s, wb, out):
+    nc = tc.nc
+    x_rows = x_bytes.rearrange("(p i) k -> p i k", i=TILES)
+    out_rows = out.rearrange("(p i) f -> p i f", i=TILES)
+    with ExitStack() as ctx:
+        keep = ctx.enter_context(tc.tile_pool(name="keep", bufs=1))
+        sb = ctx.enter_context(tc.tile_pool(name="sb", bufs=3))
+        ps = ctx.enter_context(tc.psum_pool(name="ps", bufs=2))
+        ctx.enter_context(tc.manual_schedule())
+
+        warm = keep.tile([P, 1], F32)
+        nc.vector.memset(warm[:], 0.0)
+        warm_out = keep.tile([P, 1], F32)
+        scale_bc = keep.tile([P, D], F32)
+        nc.scalar.dma_start(out=scale_bc[:], in_=x_scale.rearrange("o k -> (o k)").partition_broadcast(P))
+        nc.scalar.activation(warm_out[:], warm[:], ACT.Exp)
+
+        x_tiles = {}
+
+        def load_x(i0, n):
+            xb = keep.tile([P, n, D], U8, name="xb%d" % i0)
+            nc.sync.dma_start(out=xb[:], in_=x_rows[:, i0 : i0 + n, :])
+            for j in range(n):
+                x_tiles[i0 + j] = xb[:, j, :]
+
+        wa_raw = keep.tile([P, 2, 4, R], BF16)
+        c_rows = keep.tile([P, R], BF16)
+        nc.vector.memset(c_rows[:], 0.0)
+        s_raw = keep.tile([P, E * R], BF16)
+        w_raw = []
+
+        def load_w(w, g, n):
+            t = keep.tile([P, 4, 512], BF16, name="wraw%d" % len(w_raw))
+            nc.sync.dma_start(
+                out=t[:],
+                in_=w[512 * g : 512 * (g + 1), 512 * n : 512 * (n + 1)].rearrange("(p j) f -> p j f", j=4),
+            )
+            w_raw.append(t)
+
+        load_x(0, 1)
+        load_x(1, 1)
+        nc.sync.dma_start(out=wa_raw[:], in_=wa.rearrange("(g p j) r -> p g j r", p=P, j=4))
+        nc.sync.dma_start(out=c_rows[0:E, :], in_=c)
+        load_x(2, 2)
+        for n in range(2):
+            for g in range(2):
+                load_w(w0, g, n)
+        nc.sync.dma_start(out=s_raw[:], in_=s.partition_broadcast(P))
+        load_x(4, 4)
+        for n in range(2):
+            for g in range(2):
+                load_w(wb, g, n)
+        load_x(8, 4)
+        load_x(12, 4)
+
+        ident = keep.tile([P, P], F32)
+        make_identity(nc, ident[:])
+        ones = keep.tile([P, P], F32)
+        nc.gpsimd.memset(ones[:], 1.0)
+
+        w_codes = [keep.tile([P, 512], U32, name="wc%d" % i, align_bytes=64) for i in range(8)]
+        w_scales = [keep.tile([P, 512], U8, name="wsc%d" % i, align_bytes=64) for i in range(8)]
+        w_grp = {}
+
+        def w_copy(i):
+            t = sb.tile([P, 2048], BF16, name="wgrp", align_bytes=64, bufs=3)
+            w_grp[i] = t
+            o = t[:].rearrange("p (n j) -> p n j", j=4)
+            src = w_raw[i][:].rearrange("p j n -> p n j")
+            if W_PLAN[i][0] == "v":
+                nc.vector.tensor_copy(out=o, in_=src)
+            else:
+                nc.scalar.copy(out=o, in_=src)
+
+        def w_quant(i):
+            nc.vector.quantize_mx(out=w_codes[i][:].bitcast(FP8X4), scales=w_scales[i][:], in_=w_grp[i][:])
+
+        wa_codes = keep.tile([P, 2 * R], U32, align_bytes=64)
+        wa_scales = keep.tile([P, 2 * R], U8, align_bytes=64)
+        wa_grp = keep.tile([P, 2 * R * 4], BF16, align_bytes=64)
+        c_perm = keep.tile([P, R], F32)
+        cT = keep.tile([P, E], F32)
+        c2 = keep.tile([P, E], F32)
+        s_bc = keep.tile([P, E, R], BF16)
+
+        def wa_prep():
+            o = wa_grp[:].rearrange("p (g u q e j) -> p g u q e j", g=2, u=2, q=32, e=2)
+            for g in range(2):
+                for u in range(2):
+                    nc.vector.tensor_copy(
+                        out=o[:, g, u],
+                        in_=wa_raw[:, g].rearrange("p j (q u e) -> p u q e j", u=2, e=2)[:, u],
+                    )
+
+        def wa_quant():
+            nc.vector.quantize_mx(out=wa_codes[:].bitcast(FP8X4), scales=wa_scales[:], in_=wa_grp[:])
+
+        def c_prep():
+            nc.vector.tensor_scalar(
+                out=c_perm[:].rearrange("p (u q e) -> p u q e", u=2, e=2),
+                in0=c_rows[:].rearrange("p (q u e) -> p u q e", u=2, e=2),
+                scalar1=-0.125, scalar2=None, op0=ALU.mult,
+            )
+            ct = ps.tile([P, 512], F32, name="ab")
+            nc.tensor.transpose(ct[:, 0:P], c_perm[:], ident[:])
+            nc.vector.tensor_copy(out=cT[:], in_=ct[:, 0:E])
+            nc.vector.scalar_tensor_tensor(out=c2[:], in0=cT[:], scalar=4.0, in1=cT[:], op0=ALU.mult, op1=ALU.mult)
+
+        def s_prep():
+            o = s_bc[:].rearrange("p x (u q e) -> p x u q e", u=2, e=2)
+            i = s_raw[:].rearrange("p (x q u e) -> p x u q e", x=E, u=2, e=2)
+            for u in range(2):
+                nc.gpsimd.tensor_copy(out=o[:, :, u], in_=i[:, :, u])
+
+        st = {}
+
+        def widen(i):
+            t = sb.tile([P, D], BF16, name="xw", align_bytes=64)
+            nc.vector.tensor_tensor(out=t[:], in0=x_tiles[i].bitcast(FP8), in1=scale_bc[:], op=ALU.mult)
+            st["xw", i] = t
+
+        def turn(key, i, step):
+            tr = ps.tile([P, 4, P], F32, name="tr")
+            words = st[key, i][:].bitcast(F32)
+            for g in range(2):
+                for u in range(2):
+                    if step == 2:
+                        w = words[:, 256 * g + u : 256 * (g + 1) : 2]
+                    else:
+                        w = words[:, 256 * g + 128 * u : 256 * g + 128 * (u + 1)]
+                    nc.tensor.transpose(tr[:, 2 * g + u, :], w, ident[:])
+            st[key + "t", i] = tr
+
+        def empty(key, i):
+            t = sb.tile([P, D], BF16, name=key + "g", align_bytes=64)
+            nc.scalar.copy(
+                out=t[:].bitcast(F32).rearrange("p (g r u) -> p g r u", g=2, u=2),
+                in_=st[key + "t", i][:].rearrange("p (g u) r -> p g r u", g=2),
+            )
+            st[key + "g", i] = t
+
+        def quant(key, i, bufs):
+            cd = sb.tile([P, 256], U32, name=key + "c", align_bytes=64, bufs=bufs)
+            sc = sb.tile([P, 256], U8, name=key + "s", align_bytes=64, bufs=bufs)
+            nc.vector.quantize_mx(out=cd[:].bitcast(FP8X4), scales=sc[:], in_=st[key + "g", i][:])
+            st[key + "c", i] = (cd, sc)
+
+        def mx(o, l, r, lsl, rsl, start, stop):
+            nc.tensor.matmul_mx(
+                out=o, lhsT=l[0][:, lsl].bitcast(FP8X4), lhsT_scale=l[1][:, lsl],
+                rhs=r[0][:, rsl].bitcast(FP8X4), rhs_scale=r[1][:, rsl], start=start, stop=stop,
+            )
+
+        wa_q = (wa_codes, wa_scales)
+
+        def low_rank(i):
+            ab = ps.tile([P, 512], F32, name="ab")
+            st["ab", i] = ab
+            xq = st["xwc", i]
+            for g in range(2):
+                sl = slice(128 * g, 128 * (g + 1))
+                mx(ab[:, 0:P], wa_q, xq, sl, sl, g == 0, g == 1)
+            for g in range(2):
+                sl = slice(128 * g, 128 * (g + 1))
+                mx(ab[:, P : 2 * P], xq, wa_q, sl, sl, g == 0, g == 1)
+
+        def aT_out(i):
+            t = sb.tile([P, P], F32, name="aT", bufs=2)
+            nc.scalar.copy(out=t[:], in_=st["ab", i][:, 0:P])
+            st["aT", i] = t
+
+        def logits(i):
+            o = st["ab", i][:, 256 : 256 + E]
+            nc.tensor.matmul(o, lhsT=ones[:], rhs=c2[:], start=True, stop=False)
+            nc.tensor.matmul(o, lhsT=st["aT", i][:], rhs=cT[:], start=False, stop=True)
+
+        def row_min(i):
+            m = sb.tile([P, 1], F32, name="mn")
+            nc.vector.tensor_reduce(out=m[:], in_=st["ab", i][:, 256 : 256 + E], axis=AX.X, op=ALU.min)
+            st["mn", i] = m
+
+        def exps(i):
+            e = sb.tile([P, E], F32, name="e")
+            z = sb.tile([P, 1], F32, name="z")
+            nc.scalar.activation(
+                e[:], st["ab", i][:, 256 : 256 + E], ACT.Exp, bias=st["mn", i][:], scale=-1.0, accum_out=z[:]
+            )
+            st["e", i] = (e, z)
+
+        def recip(i):
+            r = sb.tile([P, 1], F32, name="rz")
+            nc.vector.reciprocal(out=r[:], in_=st["e", i][1][:])
+            st["rz", i] = r
+
+        def gates(i):
+            g = sb.tile([P, E], F32, name="g")
+            nc.scalar.activation(g[:], st["e", i][0][:], ACT.Copy, scale=st["rz", i][:])
+            st["g", i] = g
+
+        def zs(i):
+            t = sb.tile([P, E * R], BF16, name="z0", align_bytes=64)
+            o = t[:].rearrange("p (h u m r) -> p h m u r", h=2, u=2, m=4)
+            a = st["ab", i][:, P : 2 * P].rearrange("p (u r) -> p u r", u=2)
+            for e in range(E):
+                nc.vector.scalar_tensor_tensor(
+                    out=o[:, e // 4, e % 4], in0=a, scalar=st["g", i][:, e : e + 1],
+                    in1=s_bc[:, e, :].rearrange("p (u r) -> p u r", u=2), op0=ALU.mult, op1=ALU.mult,
+                )
+            st["z0", i] = t
+
+        def product(name, codes, i, first):
+            for n in range(2):
+                acc = ps.tile([P, 512], F32, name=name)
+                for g in range(2):
+                    w = first + 2 * n + g
+                    mx(acc[:], st[codes, i], (w_codes[w], w_scales[w]), slice(128 * g, 128 * (g + 1)), slice(0, 512), g == 0, g == 1)
+                st[name, i, n] = acc
+
+        def base_out(i):
+            t = sb.tile([P, F], F32, name="bsb", bufs=LOW_LAG - BASE_LAG + 2)
+            for n in range(2):
+                nc.scalar.copy(out=t[:, 512 * n : 512 * (n + 1)], in_=st["base", i, n][:])
+            st["bsb", i] = t
+
+        def finish(i):
+            t = sb.tile([P, F], F32, name="res", bufs=3)
+            for n in range(2):
+                sl = slice(512 * n, 512 * (n + 1))
+                nc.vector.scalar_tensor_tensor(
+                    out=t[:, sl], in0=st["low", i, n][:], scalar=1.5, in1=st["bsb", i][:, sl], op0=ALU.mult, op1=ALU.add
+                )
+                if i == TILES - 1:
+                    nc.sync.dma_start(out=out_rows[:, i, sl], in_=t[:, sl])
+            if i < TILES - 1:
+                nc.sync.dma_start(out=out_rows[:, i, :], in_=t[:])
+
+        def ok(i):
+            return 0 <= i < TILES
+
+        def run(k):
+            chunks = [i for i in range(8) if W_PLAN[i][1] == k]
+            old = [i for i in range(8) if W_PLAN[i][1] == k - 1]
+            if ok(k):
+                quant("xw", k, 8)
+            if ok(k - 2):
+                turn("z0", k - 2, 1)
+            if ok(k + 1):
+                turn("xw", k + 1, 2)
+            if ok(k - 1):
+                row_min(k - 1)
+            if ok(k - 2):
+                empty("z0", k - 2)
+            if ok(k + 2):
+                widen(k + 2)
+            if k == -2:
+                wa_prep()
+                c_prep()
+                wa_quant()
+                s_prep()
+            if ok(k - 1):
+                exps(k - 1)
+                recip(k - 1)
+            if ok(k + 1):
+                empty("xw", k + 1)
+            if ok(k):
+                low_rank(k)
+                aT_out(k)
+            if ok(k - 1):
+                gates(k - 1)
+            if ok(k - BASE_LAG):
+                product("base", "xwc", k - BASE_LAG, 0)
+            if ok(k):
+                logits(k)
+            if ok(k - BASE_LAG):
+                base_out(k - BASE_LAG)
+            if ok(k - 2):
+                quant("z0", k - 2, LOW_LAG + 1)
+            for i in chunks:
+                w_copy(i)
+            if ok(k - 1):
+                zs(k - 1)
+            for i in old:
+                w_quant(i)
+            if ok(k - LOW_LAG):
+                product("low", "z0c", k - LOW_LAG, 4)
+                finish(k - LOW_LAG)
+
+        for k in range(-2, TILES + LOW_LAG):
+            run(k)

@@ -19,9 +19,9 @@ AX = mybir.AxisListType
 P = 128
 TILES = T // P
 X_GROUPS = [(0, 1), (1, 1), (2, 2), (4, 4), (8, 4), (12, 4)]
-BASE_LAG = 3
-LOW_LAG = 7
-W_PLAN = [("v", -2), ("s", -2), ("v", -1), ("s", -1), ("s", 0), ("s", 1), ("s", 2), ("s", 3)]
+LAST = 6
+ORDER = [("zT", 5), ("xq", 0), ("xT", -1), ("widen", -2), ("logits", 1), ("zout", 5), ("xout", -1), ("low0", 6), ("base0", 2), ("add", 1), ("wq", 0), ("base1", 2), ("lr", 0), ("recip", 2), ("zq", 5), ("about", 0), ("min", 1), ("fin0", 6), ("exps", 1), ("prep", 0), ("w", 0), ("zs", 3), ("bout0", 2), ("low1", 6), ("gates", 2), ("bout1", 2), ("fin1", 6)]
+W_PLAN = {0: [(2, 1, "v"), (3, 0, "s"), (4, 0, "s")], 1: [(3, 1, "s"), (5, 0, "s"), (5, 1, "v")], 2: [], 3: [(4, 1, "s")], 4: [(6, 0, "s"), (6, 1, "v"), (7, 0, "v"), (7, 1, "v")], 5: [], -2: [(0, 0, "s"), (0, 1, "v"), (1, 0, "s")], -1: [(1, 1, "s"), (2, 0, "v")]}
 
 
 def tile_hydraloraprototyperouted_kernel(tc, x_bytes, x_scale, w0, wa, c, s, wb, out):
@@ -88,12 +88,13 @@ def tile_hydraloraprototyperouted_kernel(tc, x_bytes, x_scale, w0, wa, c, s, wb,
         w_scales = [keep.tile([P, 512], U8, name="wsc%d" % i, align_bytes=64) for i in range(8)]
         w_grp = {}
 
-        def w_copy(i):
-            t = sb.tile([P, 2048], BF16, name="wgrp", align_bytes=64, bufs=3)
-            w_grp[i] = t
-            o = t[:].rearrange("p (n j) -> p n j", j=4)
-            src = w_raw[i][:].rearrange("p j n -> p n j")
-            if W_PLAN[i][0] == "v":
+        def w_copy(i, half, eng):
+            if half == 0:
+                w_grp[i] = sb.tile([P, 2048], BF16, name="wgrp", align_bytes=64, bufs=4)
+            cols = slice(256 * half, 256 * (half + 1))
+            o = w_grp[i][:].rearrange("p (n j) -> p n j", j=4)[:, cols].rearrange("p (k i) j -> p k j i", i=4)
+            src = w_raw[i][:, :, cols].rearrange("p j (k i) -> p k j i", i=4)
+            if eng == "v":
                 nc.vector.tensor_copy(out=o, in_=src)
             else:
                 nc.scalar.copy(out=o, in_=src)
@@ -107,6 +108,7 @@ def tile_hydraloraprototyperouted_kernel(tc, x_bytes, x_scale, w0, wa, c, s, wb,
         c_perm = keep.tile([P, R], F32)
         cT = keep.tile([P, E], F32)
         c2 = keep.tile([P, E], F32)
+        c2_bc = keep.tile([P, E], F32)
         s_bc = keep.tile([P, E, R], BF16)
 
         def wa_prep():
@@ -127,10 +129,15 @@ def tile_hydraloraprototyperouted_kernel(tc, x_bytes, x_scale, w0, wa, c, s, wb,
                 in0=c_rows[:].rearrange("p (q u e) -> p u q e", u=2, e=2),
                 scalar1=-0.125, scalar2=None, op0=ALU.mult,
             )
-            ct = ps.tile([P, 512], F32, name="ab")
-            nc.tensor.transpose(ct[:, 0:P], c_perm[:], ident[:])
-            nc.vector.tensor_copy(out=cT[:], in_=ct[:, 0:E])
+            ct = ps.tile([P, 4, P], F32, name="tr")
+            nc.tensor.transpose(ct[:, 0, :], c_perm[:], ident[:])
+            nc.vector.tensor_copy(out=cT[:], in_=ct[:, 0, 0:E])
             nc.vector.scalar_tensor_tensor(out=c2[:], in0=cT[:], scalar=4.0, in1=cT[:], op0=ALU.mult, op1=ALU.mult)
+
+        def c2_prep():
+            o = ps.tile([P, E], F32, name="lg", bufs=1)
+            nc.tensor.matmul(o[:], lhsT=ones[:], rhs=c2[:], start=True, stop=True)
+            nc.vector.tensor_copy(out=c2_bc[:], in_=o[:])
 
         def s_prep():
             o = s_bc[:].rearrange("p x (u q e) -> p x u q e", u=2, e=2)
@@ -180,7 +187,7 @@ def tile_hydraloraprototyperouted_kernel(tc, x_bytes, x_scale, w0, wa, c, s, wb,
         wa_q = (wa_codes, wa_scales)
 
         def low_rank(i):
-            ab = ps.tile([P, 512], F32, name="ab")
+            ab = ps.tile([P, 2 * P], F32, name="ab", bufs=1)
             st["ab", i] = ab
             xq = st["xwc", i]
             for g in range(2):
@@ -190,26 +197,31 @@ def tile_hydraloraprototyperouted_kernel(tc, x_bytes, x_scale, w0, wa, c, s, wb,
                 sl = slice(128 * g, 128 * (g + 1))
                 mx(ab[:, P : 2 * P], xq, wa_q, sl, sl, g == 0, g == 1)
 
-        def aT_out(i):
-            t = sb.tile([P, P], F32, name="aT", bufs=2)
-            nc.scalar.copy(out=t[:], in_=st["ab", i][:, 0:P])
-            st["aT", i] = t
+        def ab_out(i):
+            t = sb.tile([P, 2 * P], F32, name="ab_sb", bufs=4)
+            nc.scalar.copy(out=t[:], in_=st["ab", i][:])
+            st["ab_sb", i] = t
 
         def logits(i):
-            o = st["ab", i][:, 256 : 256 + E]
-            nc.tensor.matmul(o, lhsT=ones[:], rhs=c2[:], start=True, stop=False)
-            nc.tensor.matmul(o, lhsT=st["aT", i][:], rhs=cT[:], start=False, stop=True)
+            o = ps.tile([P, E], F32, name="lg", bufs=1)
+            nc.tensor.matmul(o[:], lhsT=st["ab_sb", i][:, 0:P], rhs=cT[:], start=True, stop=True)
+            st["lg", i] = o
+
+        def add_c2(i):
+            t = sb.tile([P, E], F32, name="nl")
+            nc.vector.tensor_tensor(out=t[:], in0=st["lg", i][:], in1=c2_bc[:], op=ALU.add)
+            st["nl", i] = t
 
         def row_min(i):
             m = sb.tile([P, 1], F32, name="mn")
-            nc.vector.tensor_reduce(out=m[:], in_=st["ab", i][:, 256 : 256 + E], axis=AX.X, op=ALU.min)
+            nc.vector.tensor_reduce(out=m[:], in_=st["nl", i][:], axis=AX.X, op=ALU.min)
             st["mn", i] = m
 
         def exps(i):
             e = sb.tile([P, E], F32, name="e")
             z = sb.tile([P, 1], F32, name="z")
             nc.scalar.activation(
-                e[:], st["ab", i][:, 256 : 256 + E], ACT.Exp, bias=st["mn", i][:], scale=-1.0, accum_out=z[:]
+                e[:], st["nl", i][:], ACT.Exp, bias=st["mn", i][:], scale=-1.0, accum_out=z[:]
             )
             st["e", i] = (e, z)
 
@@ -226,90 +238,70 @@ def tile_hydraloraprototyperouted_kernel(tc, x_bytes, x_scale, w0, wa, c, s, wb,
         def zs(i):
             t = sb.tile([P, E * R], BF16, name="z0", align_bytes=64)
             o = t[:].rearrange("p (h u m r) -> p h m u r", h=2, u=2, m=4)
-            a = st["ab", i][:, P : 2 * P].rearrange("p (u r) -> p u r", u=2)
-            for e in range(E):
+            a = st["ab_sb", i][:, P : 2 * P].rearrange("p (u r) -> p u r", u=2)
+            for e in (0, 4, 1, 5, 2, 6, 3, 7):
                 nc.vector.scalar_tensor_tensor(
                     out=o[:, e // 4, e % 4], in0=a, scalar=st["g", i][:, e : e + 1],
                     in1=s_bc[:, e, :].rearrange("p (u r) -> p u r", u=2), op0=ALU.mult, op1=ALU.mult,
                 )
             st["z0", i] = t
 
-        def product(name, codes, i, first):
-            for n in range(2):
-                acc = ps.tile([P, 512], F32, name=name)
-                for g in range(2):
-                    w = first + 2 * n + g
-                    mx(acc[:], st[codes, i], (w_codes[w], w_scales[w]), slice(128 * g, 128 * (g + 1)), slice(0, 512), g == 0, g == 1)
-                st[name, i, n] = acc
+        def product_half(name, codes, i, first, n):
+            acc = ps.tile([P, 512], F32, name="acc", bufs=4)
+            for g in range(2):
+                w = first + 2 * n + g
+                mx(acc[:], st[codes, i], (w_codes[w], w_scales[w]), slice(128 * g, 128 * (g + 1)), slice(0, 512), g == 0, g == 1)
+            st[name, i, n] = acc
 
-        def base_out(i):
-            t = sb.tile([P, F], F32, name="bsb", bufs=LOW_LAG - BASE_LAG + 2)
-            for n in range(2):
-                nc.scalar.copy(out=t[:, 512 * n : 512 * (n + 1)], in_=st["base", i, n][:])
-            st["bsb", i] = t
+        def base_out(i, n):
+            if n == 0:
+                st["bsb", i] = sb.tile([P, F], F32, name="bsb", bufs=6)
+            nc.scalar.copy(out=st["bsb", i][:, 512 * n : 512 * (n + 1)], in_=st["base", i, n][:])
 
-        def finish(i):
-            t = sb.tile([P, F], F32, name="res", bufs=3)
-            for n in range(2):
-                sl = slice(512 * n, 512 * (n + 1))
-                nc.vector.scalar_tensor_tensor(
-                    out=t[:, sl], in0=st["low", i, n][:], scalar=1.5, in1=st["bsb", i][:, sl], op0=ALU.mult, op1=ALU.add
-                )
-                if i == TILES - 1:
-                    nc.sync.dma_start(out=out_rows[:, i, sl], in_=t[:, sl])
-            if i < TILES - 1:
+        def finish(i, n):
+            if n == 0:
+                st["res", i] = sb.tile([P, F], F32, name="res", bufs=5)
+            t = st["res", i]
+            sl = slice(512 * n, 512 * (n + 1))
+            nc.vector.scalar_tensor_tensor(
+                out=t[:, sl], in0=st["low", i, n][:], scalar=1.5, in1=st["bsb", i][:, sl], op0=ALU.mult, op1=ALU.add
+            )
+            if i == TILES - 1:
+                nc.sync.dma_start(out=out_rows[:, i, sl], in_=t[:, sl])
+            elif n == 1:
                 nc.sync.dma_start(out=out_rows[:, i, :], in_=t[:])
 
         def ok(i):
             return 0 <= i < TILES
 
-        def run(k):
-            chunks = [i for i in range(8) if W_PLAN[i][1] == k]
-            old = [i for i in range(8) if W_PLAN[i][1] == k - 1]
-            if ok(k):
-                quant("xw", k, 8)
-            if ok(k - 2):
-                turn("z0", k - 2, 1)
-            if ok(k + 1):
-                turn("xw", k + 1, 2)
-            if ok(k - 1):
-                row_min(k - 1)
-            if ok(k - 2):
-                empty("z0", k - 2)
-            if ok(k + 2):
-                widen(k + 2)
-            if k == -2:
-                wa_prep()
-                c_prep()
-                wa_quant()
-                s_prep()
-            if ok(k - 1):
-                exps(k - 1)
-                recip(k - 1)
-            if ok(k + 1):
-                empty("xw", k + 1)
-            if ok(k):
-                low_rank(k)
-                aT_out(k)
-            if ok(k - 1):
-                gates(k - 1)
-            if ok(k - BASE_LAG):
-                product("base", "xwc", k - BASE_LAG, 0)
-            if ok(k):
-                logits(k)
-            if ok(k - BASE_LAG):
-                base_out(k - BASE_LAG)
-            if ok(k - 2):
-                quant("z0", k - 2, LOW_LAG + 1)
-            for i in chunks:
-                w_copy(i)
-            if ok(k - 1):
-                zs(k - 1)
-            for i in old:
-                w_quant(i)
-            if ok(k - LOW_LAG):
-                product("low", "z0c", k - LOW_LAG, 4)
-                finish(k - LOW_LAG)
+        ops = {
+            "recip": recip, "gates": gates, "zT": lambda i: turn("z0", i, 1), "xT": lambda i: turn("xw", i, 2), "logits": logits,
+            "xq": lambda i: quant("xw", i, 8), "zout": lambda i: empty("z0", i), "xout": lambda i: empty("xw", i),
+            "add": add_c2, "widen": widen, "min": row_min, "exps": exps, "zq": lambda i: quant("z0", i, 12),
+            "lr": low_rank, "about": ab_out, "base0": lambda i: product_half("base", "xwc", i, 0, 0), "base1": lambda i: product_half("base", "xwc", i, 0, 1),
+            "bout0": lambda i: base_out(i, 0), "bout1": lambda i: base_out(i, 1),
+            "low0": lambda i: product_half("low", "z0c", i, 4, 0), "low1": lambda i: product_half("low", "z0c", i, 4, 1),
+            "zs": zs, "fin0": lambda i: finish(i, 0), "fin1": lambda i: finish(i, 1),
+        }
 
-        for k in range(-2, TILES + LOW_LAG):
+        def run(k):
+            for name, lag in ORDER:
+                if name == "w":
+                    for c in W_PLAN.get(k, []):
+                        w_copy(*c)
+                elif name == "wq":
+                    for c in W_PLAN.get(k - 1, []):
+                        if c[1] == 1:
+                            w_quant(c[0])
+                elif name == "prep":
+                    if k == -2:
+                        wa_prep()
+                        c_prep()
+                        wa_quant()
+                        s_prep()
+                        c2_prep()
+                elif ok(k - lag):
+                    ops[name](k - lag)
+
+        for k in range(-2, TILES + LAST):
             run(k)

from contextlib import ExitStack

import concourse.mybir as mybir
from concourse.masks import make_identity

T, D, F, R, E = 2048, 1024, 1024, 128, 8
FLOPS = 2 * T * D * (F + R) + 2 * T * E * R * F

F32 = mybir.dt.float32
BF16 = mybir.dt.bfloat16
U32 = mybir.dt.uint32
U8 = mybir.dt.uint8
FP8 = mybir.dt.float8_e4m3fn
FP8X4 = mybir.dt.float8_e4m3fn_x4
ALU = mybir.AluOpType
ACT = mybir.ActivationFunctionType
AX = mybir.AxisListType

P = 128
TILES = T // P
X_GROUPS = [(0, 1), (1, 1), (2, 2), (4, 4), (8, 4), (12, 4)]
LAST = 6
ORDER = [("zT", 5), ("xq", 0), ("xT", -1), ("widen", -2), ("logits", 1), ("zout", 5), ("xout", -1), ("low0", 6), ("base0", 2), ("add", 1), ("wq", 0), ("base1", 2), ("lr", 0), ("recip", 2), ("zq", 5), ("about", 0), ("min", 1), ("fin0", 6), ("exps", 1), ("prep", 0), ("w", 0), ("zs", 3), ("bout0", 2), ("low1", 6), ("gates", 2), ("bout1", 2), ("fin1", 6)]
W_PLAN = {0: [(2, 1, "v"), (3, 0, "s"), (4, 0, "s")], 1: [(3, 1, "s"), (5, 0, "s"), (5, 1, "v")], 2: [], 3: [(4, 1, "s")], 4: [(6, 0, "s"), (6, 1, "v"), (7, 0, "v"), (7, 1, "v")], 5: [], -2: [(0, 0, "s"), (0, 1, "v"), (1, 0, "s")], -1: [(1, 1, "s"), (2, 0, "v")]}


def tile_hydraloraprototyperouted_kernel(tc, x_bytes, x_scale, w0, wa, c, s, wb, out):
    nc = tc.nc
    x_rows = x_bytes.rearrange("(p i) k -> p i k", i=TILES)
    out_rows = out.rearrange("(p i) f -> p i f", i=TILES)
    with ExitStack() as ctx:
        keep = ctx.enter_context(tc.tile_pool(name="keep", bufs=1))
        sb = ctx.enter_context(tc.tile_pool(name="sb", bufs=3))
        ps = ctx.enter_context(tc.psum_pool(name="ps", bufs=2))
        ctx.enter_context(tc.manual_schedule())

        warm = keep.tile([P, 1], F32)
        nc.vector.memset(warm[:], 0.0)
        warm_out = keep.tile([P, 1], F32)
        scale_bc = keep.tile([P, D], F32)
        nc.scalar.dma_start(out=scale_bc[:], in_=x_scale.rearrange("o k -> (o k)").partition_broadcast(P))
        nc.scalar.activation(warm_out[:], warm[:], ACT.Exp)

        x_tiles = {}

        def load_x(i0, n):
            xb = keep.tile([P, n, D], U8, name="xb%d" % i0)
            nc.sync.dma_start(out=xb[:], in_=x_rows[:, i0 : i0 + n, :])
            for j in range(n):
                x_tiles[i0 + j] = xb[:, j, :]

        wa_raw = keep.tile([P, 2, 4, R], BF16)
        c_rows = keep.tile([P, R], BF16)
        nc.vector.memset(c_rows[:], 0.0)
        s_raw = keep.tile([P, E * R], BF16)
        w_raw = []

        def load_w(w, g, n):
            t = keep.tile([P, 4, 512], BF16, name="wraw%d" % len(w_raw))
            nc.sync.dma_start(
                out=t[:],
                in_=w[512 * g : 512 * (g + 1), 512 * n : 512 * (n + 1)].rearrange("(p j) f -> p j f", j=4),
            )
            w_raw.append(t)

        load_x(0, 1)
        load_x(1, 1)
        nc.sync.dma_start(out=wa_raw[:], in_=wa.rearrange("(g p j) r -> p g j r", p=P, j=4))
        nc.sync.dma_start(out=c_rows[0:E, :], in_=c)
        load_x(2, 2)
        for n in range(2):
            for g in range(2):
                load_w(w0, g, n)
        nc.sync.dma_start(out=s_raw[:], in_=s.partition_broadcast(P))
        load_x(4, 4)
        for n in range(2):
            for g in range(2):
                load_w(wb, g, n)
        load_x(8, 4)
        load_x(12, 4)

        ident = keep.tile([P, P], F32)
        make_identity(nc, ident[:])
        ones = keep.tile([P, P], F32)
        nc.gpsimd.memset(ones[:], 1.0)

        w_codes = [keep.tile([P, 512], U32, name="wc%d" % i, align_bytes=64) for i in range(8)]
        w_scales = [keep.tile([P, 512], U8, name="wsc%d" % i, align_bytes=64) for i in range(8)]
        w_grp = {}

        def w_copy(i, half, eng):
            if half == 0:
                w_grp[i] = sb.tile([P, 2048], BF16, name="wgrp", align_bytes=64, bufs=4)
            cols = slice(256 * half, 256 * (half + 1))
            o = w_grp[i][:].rearrange("p (n j) -> p n j", j=4)[:, cols].rearrange("p (k i) j -> p k j i", i=4)
            src = w_raw[i][:, :, cols].rearrange("p j (k i) -> p k j i", i=4)
            if eng == "v":
                nc.vector.tensor_copy(out=o, in_=src)
            else:
                nc.scalar.copy(out=o, in_=src)

        def w_quant(i):
            nc.vector.quantize_mx(out=w_codes[i][:].bitcast(FP8X4), scales=w_scales[i][:], in_=w_grp[i][:])

        wa_codes = keep.tile([P, 2 * R], U32, align_bytes=64)
        wa_scales = keep.tile([P, 2 * R], U8, align_bytes=64)
        wa_grp = keep.tile([P, 2 * R * 4], BF16, align_bytes=64)
        c_perm = keep.tile([P, R], F32)
        cT = keep.tile([P, E], F32)
        c2 = keep.tile([P, E], F32)
        c2_bc = keep.tile([P, E], F32)
        s_bc = keep.tile([P, E, R], BF16)

        def wa_prep():
            o = wa_grp[:].rearrange("p (g u q e j) -> p g u q e j", g=2, u=2, q=32, e=2)
            for g in range(2):
                for u in range(2):
                    nc.vector.tensor_copy(
                        out=o[:, g, u],
                        in_=wa_raw[:, g].rearrange("p j (q u e) -> p u q e j", u=2, e=2)[:, u],
                    )

        def wa_quant():
            nc.vector.quantize_mx(out=wa_codes[:].bitcast(FP8X4), scales=wa_scales[:], in_=wa_grp[:])

        def c_prep():
            nc.vector.tensor_scalar(
                out=c_perm[:].rearrange("p (u q e) -> p u q e", u=2, e=2),
                in0=c_rows[:].rearrange("p (q u e) -> p u q e", u=2, e=2),
                scalar1=-0.125, scalar2=None, op0=ALU.mult,
            )
            ct = ps.tile([P, 4, P], F32, name="tr")
            nc.tensor.transpose(ct[:, 0, :], c_perm[:], ident[:])
            nc.vector.tensor_copy(out=cT[:], in_=ct[:, 0, 0:E])
            nc.vector.scalar_tensor_tensor(out=c2[:], in0=cT[:], scalar=4.0, in1=cT[:], op0=ALU.mult, op1=ALU.mult)

        def c2_prep():
            o = ps.tile([P, E], F32, name="lg", bufs=1)
            nc.tensor.matmul(o[:], lhsT=ones[:], rhs=c2[:], start=True, stop=True)
            nc.vector.tensor_copy(out=c2_bc[:], in_=o[:])

        def s_prep():
            o = s_bc[:].rearrange("p x (u q e) -> p x u q e", u=2, e=2)
            i = s_raw[:].rearrange("p (x q u e) -> p x u q e", x=E, u=2, e=2)
            for u in range(2):
                nc.gpsimd.tensor_copy(out=o[:, :, u], in_=i[:, :, u])

        st = {}

        def widen(i):
            t = sb.tile([P, D], BF16, name="xw", align_bytes=64)
            nc.vector.tensor_tensor(out=t[:], in0=x_tiles[i].bitcast(FP8), in1=scale_bc[:], op=ALU.mult)
            st["xw", i] = t

        def turn(key, i, step):
            tr = ps.tile([P, 4, P], F32, name="tr")
            words = st[key, i][:].bitcast(F32)
            for g in range(2):
                for u in range(2):
                    if step == 2:
                        w = words[:, 256 * g + u : 256 * (g + 1) : 2]
                    else:
                        w = words[:, 256 * g + 128 * u : 256 * g + 128 * (u + 1)]
                    nc.tensor.transpose(tr[:, 2 * g + u, :], w, ident[:])
            st[key + "t", i] = tr

        def empty(key, i):
            t = sb.tile([P, D], BF16, name=key + "g", align_bytes=64)
            nc.scalar.copy(
                out=t[:].bitcast(F32).rearrange("p (g r u) -> p g r u", g=2, u=2),
                in_=st[key + "t", i][:].rearrange("p (g u) r -> p g r u", g=2),
            )
            st[key + "g", i] = t

        def quant(key, i, bufs):
            cd = sb.tile([P, 256], U32, name=key + "c", align_bytes=64, bufs=bufs)
            sc = sb.tile([P, 256], U8, name=key + "s", align_bytes=64, bufs=bufs)
            nc.vector.quantize_mx(out=cd[:].bitcast(FP8X4), scales=sc[:], in_=st[key + "g", i][:])
            st[key + "c", i] = (cd, sc)

        def mx(o, l, r, lsl, rsl, start, stop):
            nc.tensor.matmul_mx(
                out=o, lhsT=l[0][:, lsl].bitcast(FP8X4), lhsT_scale=l[1][:, lsl],
                rhs=r[0][:, rsl].bitcast(FP8X4), rhs_scale=r[1][:, rsl], start=start, stop=stop,
            )

        wa_q = (wa_codes, wa_scales)

        def low_rank(i):
            ab = ps.tile([P, 2 * P], F32, name="ab", bufs=1)
            st["ab", i] = ab
            xq = st["xwc", i]
            for g in range(2):
                sl = slice(128 * g, 128 * (g + 1))
                mx(ab[:, 0:P], wa_q, xq, sl, sl, g == 0, g == 1)
            for g in range(2):
                sl = slice(128 * g, 128 * (g + 1))
                mx(ab[:, P : 2 * P], xq, wa_q, sl, sl, g == 0, g == 1)

        def ab_out(i):
            t = sb.tile([P, 2 * P], F32, name="ab_sb", bufs=4)
            nc.scalar.copy(out=t[:], in_=st["ab", i][:])
            st["ab_sb", i] = t

        def logits(i):
            o = ps.tile([P, E], F32, name="lg", bufs=1)
            nc.tensor.matmul(o[:], lhsT=st["ab_sb", i][:, 0:P], rhs=cT[:], start=True, stop=True)
            st["lg", i] = o

        def add_c2(i):
            t = sb.tile([P, E], F32, name="nl")
            nc.vector.tensor_tensor(out=t[:], in0=st["lg", i][:], in1=c2_bc[:], op=ALU.add)
            st["nl", i] = t

        def row_min(i):
            m = sb.tile([P, 1], F32, name="mn")
            nc.vector.tensor_reduce(out=m[:], in_=st["nl", i][:], axis=AX.X, op=ALU.min)
            st["mn", i] = m

        def exps(i):
            e = sb.tile([P, E], F32, name="e")
            z = sb.tile([P, 1], F32, name="z")
            nc.scalar.activation(
                e[:], st["nl", i][:], ACT.Exp, bias=st["mn", i][:], scale=-1.0, accum_out=z[:]
            )
            st["e", i] = (e, z)

        def recip(i):
            r = sb.tile([P, 1], F32, name="rz")
            nc.vector.reciprocal(out=r[:], in_=st["e", i][1][:])
            st["rz", i] = r

        def gates(i):
            g = sb.tile([P, E], F32, name="g")
            nc.scalar.activation(g[:], st["e", i][0][:], ACT.Copy, scale=st["rz", i][:])
            st["g", i] = g

        def zs(i):
            t = sb.tile([P, E * R], BF16, name="z0", align_bytes=64)
            o = t[:].rearrange("p (h u m r) -> p h m u r", h=2, u=2, m=4)
            a = st["ab_sb", i][:, P : 2 * P].rearrange("p (u r) -> p u r", u=2)
            for e in (0, 4, 1, 5, 2, 6, 3, 7):
                nc.vector.scalar_tensor_tensor(
                    out=o[:, e // 4, e % 4], in0=a, scalar=st["g", i][:, e : e + 1],
                    in1=s_bc[:, e, :].rearrange("p (u r) -> p u r", u=2), op0=ALU.mult, op1=ALU.mult,
                )
            st["z0", i] = t

        def product_half(name, codes, i, first, n):
            acc = ps.tile([P, 512], F32, name="acc", bufs=4)
            for g in range(2):
                w = first + 2 * n + g
                mx(acc[:], st[codes, i], (w_codes[w], w_scales[w]), slice(128 * g, 128 * (g + 1)), slice(0, 512), g == 0, g == 1)
            st[name, i, n] = acc

        def base_out(i, n):
            if n == 0:
                st["bsb", i] = sb.tile([P, F], F32, name="bsb", bufs=6)
            nc.scalar.copy(out=st["bsb", i][:, 512 * n : 512 * (n + 1)], in_=st["base", i, n][:])

        def finish(i, n):
            if n == 0:
                st["res", i] = sb.tile([P, F], F32, name="res", bufs=5)
            t = st["res", i]
            sl = slice(512 * n, 512 * (n + 1))
            nc.vector.scalar_tensor_tensor(
                out=t[:, sl], in0=st["low", i, n][:], scalar=1.5, in1=st["bsb", i][:, sl], op0=ALU.mult, op1=ALU.add
            )
            if i == TILES - 1:
                nc.sync.dma_start(out=out_rows[:, i, sl], in_=t[:, sl])
            elif n == 1:
                nc.sync.dma_start(out=out_rows[:, i, :], in_=t[:])

        def ok(i):
            return 0 <= i < TILES

        ops = {
            "recip": recip, "gates": gates, "zT": lambda i: turn("z0", i, 1), "xT": lambda i: turn("xw", i, 2), "logits": logits,
            "xq": lambda i: quant("xw", i, 8), "zout": lambda i: empty("z0", i), "xout": lambda i: empty("xw", i),
            "add": add_c2, "widen": widen, "min": row_min, "exps": exps, "zq": lambda i: quant("z0", i, 12),
            "lr": low_rank, "about": ab_out, "base0": lambda i: product_half("base", "xwc", i, 0, 0), "base1": lambda i: product_half("base", "xwc", i, 0, 1),
            "bout0": lambda i: base_out(i, 0), "bout1": lambda i: base_out(i, 1),
            "low0": lambda i: product_half("low", "z0c", i, 4, 0), "low1": lambda i: product_half("low", "z0c", i, 4, 1),
            "zs": zs, "fin0": lambda i: finish(i, 0), "fin1": lambda i: finish(i, 1),
        }

        def run(k):
            for name, lag in ORDER:
                if name == "w":
                    for c in W_PLAN.get(k, []):
                        w_copy(*c)
                elif name == "wq":
                    for c in W_PLAN.get(k - 1, []):
                        if c[1] == 1:
                            w_quant(c[0])
                elif name == "prep":
                    if k == -2:
                        wa_prep()
                        c_prep()
                        wa_quant()
                        s_prep()
                        c2_prep()
                elif ok(k - lag):
                    ops[name](k - lag)

        for k in range(-2, TILES + LAST):
            run(k)
